import numpy as np
import ml_dtypes


def mxq(x, axis, fmt="e4m3"):
    dtype, down = {"e4m3": (ml_dtypes.float8_e4m3fn, 7), "e5m2": (ml_dtypes.float8_e5m2, 14)}[fmt]
    v = np.moveaxis(np.asarray(x, np.float32).astype(ml_dtypes.bfloat16).astype(np.float64), axis, -1)
    blocks = v.reshape(v.shape[:-1] + (-1, 32))
    amax = np.abs(blocks).max(-1, keepdims=True)
    byte = np.maximum(np.where(amax > 0, np.frexp(amax)[1] - 1 + 127, 0) - down, 1)
    scale = np.exp2(byte - 127.0)
    codes = (blocks / scale).astype(np.float32).astype(dtype).astype(np.float64)
    return np.moveaxis((codes * scale).reshape(v.shape), -1, axis)


WIDE = False


def mx_kscale(k):
    if not WIDE:
        return np.ones(k)
    levels = np.array([10, -10, 5, -5, 0])
    if k % 512:
        return np.exp2(np.random.permutation(np.resize(levels, k // 32))).repeat(32)
    a = np.empty((k // 512, 16))
    for p in range(k // 512):
        a[p, :8] = np.random.permutation(np.resize(levels, 8))
        for g in range(8):
            far = levels[np.abs(levels - a[p, g]) >= 10]
            a[p, g + 8] = far[np.random.randint(len(far))]
    return np.exp2(a.ravel()).repeat(32)


def f64(x):
    return np.asarray(x).astype(np.float64)


def striped(idx):
    return np.tile(idx.reshape(-1, 16).T, (8, 1)).astype(np.uint16)


def unstriped(offs):
    return offs[:16].T.reshape(-1).astype(np.int64)


E2M1 = np.array([0.0, 0.5, 1.0, 1.5, 2.0, 3.0, 4.0, 6.0, -0.0, -0.5, -1.0, -1.5, -2.0, -3.0, -4.0, -6.0])


def pack_weight(w, fmt):
    k, n = w.shape
    w = f64(np.asarray(w, np.float32).astype(ml_dtypes.bfloat16)).reshape(k // 32, 32, n)
    amax = np.abs(w).max(1)
    if fmt == "e4m3":
        byte = np.frexp(amax)[1] - 1 + 127 - 7
    else:
        mant, ex = np.frexp(amax / 6.0)
        byte = np.where(mant > 0.5, ex, ex - 1) + 127
    byte = np.clip(np.where(amax > 0, byte, 1), 1, 254)
    scaled = (w * np.exp2(127.0 - byte)[:, None, :]).reshape(k, n).astype(np.float32)
    by_word = np.ascontiguousarray(scaled.reshape(k // 512, 128, 4, n).transpose(0, 1, 3, 2))
    if fmt == "e4m3":
        words = by_word.astype(ml_dtypes.float8_e4m3fn).view(np.uint8)
    else:
        c = by_word.astype(ml_dtypes.float4_e2m1fn).view(np.uint8) & 0xF
        words = (c[..., 0::2] | (c[..., 1::2] << 4)).reshape(k // 512, 128, 2 * n)
    return np.ascontiguousarray(words), np.ascontiguousarray(byte.astype(np.uint8).reshape(k // 512, 16, n))


def unpack_weight(words, scales, fmt):
    g, _, n = scales.shape
    words = np.ascontiguousarray(words).reshape(g, 128, n, -1)
    if fmt == "e4m3":
        vals = words.view(ml_dtypes.float8_e4m3fn).astype(np.float64)
    else:
        nib = np.empty((g, 128, n, 4), np.uint8)
        nib[..., 0::2] = words & 0xF
        nib[..., 1::2] = words >> 4
        vals = E2M1[nib]
    vals = vals * np.repeat(np.exp2(scales.astype(np.float64) - 127.0), 8, axis=1)[..., None]
    return vals.transpose(0, 1, 3, 2).reshape(g * 512, n)


def gelu(v):
    return 0.5 * v * (1.0 + np.tanh(np.sqrt(2.0 / np.pi) * (v + 0.044715 * v**3)))


def bf(x):
    return np.asarray(x, np.float32).astype(ml_dtypes.bfloat16)


def planes(Y):
    n, m = Y.shape
    b = f64(bf(Y)).reshape(n // 32, 32, m)
    amax = np.abs(b).max(1)
    byte = np.clip(np.where(amax > 0, np.frexp(amax)[1] - 1 + 127 - 7, 1), 1, 254)
    codes = (b * np.exp2(127.0 - byte)[:, None, :]).reshape(n, m).astype(np.float32).astype(ml_dtypes.float8_e4m3fn).view(np.uint8)
    words = codes.reshape(n // 512, 128, 4, m).transpose(0, 1, 3, 2)
    return np.ascontiguousarray(words), np.ascontiguousarray(byte.astype(np.uint8).reshape(n // 512, 16, m))


K, T, S, H, T2, P, N = 1024, 4096, 1024, 1024, 2048, 512, 512


def setup_inputs():
    n = np.random.standard_normal
    s = mx_kscale(K)[:, None]
    u = mx_kscale(H)[:, None]
    lift = 0.35 * np.exp(0.5 * n((H, 1))) * u ** 2
    d = {}
    d["tab_words"], d["tab_scales"] = pack_weight(n((K, T)) * np.exp(0.4 * n(T)) * s, "e4m3")
    d["offs"] = striped(np.random.permutation(T)[:S])
    d["w1"] = (4.0 * n((K, H)) / K ** 0.5 / s * lift.T).astype(np.float32)
    d["lift"] = lift[:, 0].astype(np.float32)
    d["page0"] = (n((H, T2)) * u).astype(np.float32)
    d["wgs"] = np.exp(0.3 * n((128, S))).astype(np.float32)
    d["offs2"] = striped(np.random.permutation(T2)[:S])
    d["offs3"] = striped(np.random.permutation(T2)[:P])
    d["ease"] = (np.exp(0.3 * n(H)) / u[:, 0]).astype(np.float32)
    d["tgain"] = (np.exp(0.3 * n(H)) * u[:, 0]).astype(np.float32)
    d["moon"] = (n((H, P)) * u).astype(np.float32)
    d["w2"] = (1.5 * n((H, N)) / H ** 0.5 / u).astype(np.float32)
    d["wm_words"], d["wm_scales"] = pack_weight(-0.7 * n((H, N)) / H ** 0.5 / u, "e2m1")
    return d


def reference(tab_words, tab_scales, offs, w1, lift, page0, wgs, offs2, offs3, ease, tgain, moon, w2, wm_words, wm_scales):
    v = unpack_weight(tab_words, tab_scales, "e4m3")[:, unstriped(offs)]
    strip = mxq(f64(w1), 0, "e4m3").T @ v
    h = np.sqrt(f64(lift)[:, None] + np.abs(strip))
    page = f64(page0).copy()
    page[:, unstriped(offs2)] = np.tile(f64(wgs), (H // 128, 1)) * h
    x = page[:, unstriped(offs3)]
    arc = np.tanh(x * f64(ease)[:, None]) * f64(tgain)[:, None]
    lit = x + f64(moon)
    wm = unpack_weight(wm_words, wm_scales, "e2m1")
    y = mxq(f64(w2), 0, "e4m3").T @ mxq(arc, 0, "e4m3") + wm.T @ mxq(lit, 0, "e4m3")
    words, scales = planes(page)
    return y, page, words, scales

@@ -1,0 +1,382 @@
+from contextlib import ExitStack
+
+import concourse.mybir as mybir
+
+K, T, S, H, T2, PM, N = 1024, 4096, 1024, 1024, 2048, 512, 512
+FLOPS = 2 * K * H * S + 2 * 2 * H * N * PM
+
+F32 = mybir.dt.float32
+BF16 = mybir.dt.bfloat16
+I32 = mybir.dt.int32
+U32 = mybir.dt.uint32
+U16 = mybir.dt.uint16
+U8 = mybir.dt.uint8
+FP8X4 = mybir.dt.float8_e4m3fn_x4
+FP4X4 = mybir.dt.float4_e2m1fn_x4
+ACT = mybir.ActivationFunctionType
+ALU = mybir.AluOpType
+
+P = 128
+KB = 1024
+BANK = 512
+CHUNK = 512
+CHUNKS = T2 // CHUNK
+
+TAB = 0
+W1_FIRST = 32 * KB
+W1_SECOND = 48 * KB
+PAGES = 64 * KB
+WGS_SECOND = 96 * KB
+LATE_SCALES = 100 * KB
+HS = 104 * KB
+W2_RAW = 144 * KB
+WOVEN = 160 * KB
+TAB_SCALES = 176 * KB
+PICKED = 180 * KB
+STAGING = 189 * KB
+W1_CODES = 197 * KB
+W2_CODES = 207 * KB
+WM = 211 * KB
+X_FIRST = 214 * KB
+ABS = 222 * KB
+MOON_FIRST = 230 * KB
+
+
+def tile_list_auroral_arc_page_kernel(
+    tc, tab_words, tab_scales, offs, w1, lift, page0, wgs, offs2, offs3, ease, tgain, moon, w2,
+    wm_words, wm_scales, out_0, out_1, out_2, out_3,
+):
+    nc = tc.nc
+    with ExitStack() as ctx:
+        lists = ctx.enter_context(tc.tile_pool(name="lists", bufs=1))
+        sb = ctx.enter_context(tc.tile_pool(name="sb", bufs=1))
+        psum = ctx.enter_context(tc.psum_pool(name="psum", bufs=1))
+
+        def place(name, shape, dtype, offset):
+            return sb.tile(shape, dtype, name=name, offset=offset, align_bytes=64)
+
+        def rows_4p_t(matrix, g):
+            return matrix[512 * g : 512 * (g + 1), :].rearrange("(p t) c -> p t c", t=4)
+
+        idx = lists.tile([P, S // 16], U16, name="idx")
+        idx2 = lists.tile([P, S // 16], U16, name="idx2")
+        idx3 = lists.tile([P, PM // 16], U16, name="idx3")
+        lift_sb = lists.tile([P, 2, 4], F32, name="lift_sb")
+        ease_sb = lists.tile([P, 2, 4], F32, name="ease_sb")
+        tgain_sb = lists.tile([P, 2, 4], F32, name="tgain_sb")
+        warm = lists.tile([P, 2], F32, name="warm")
+
+        nc.sync.dma_start(idx[:], offs)
+        tab = []
+        for a in range(2):
+            words = place(f"tab{a}", [P, T], I32, TAB + a * 16 * KB)
+            nc.sync.dma_start(words[:], tab_words[a].rearrange("p c i -> p (c i)").bitcast(I32))
+            tab.append(words)
+            if a == 0:
+                tab_sc = place("tab_sc", [P, T], U8, TAB_SCALES)
+                nc.vector.memset(tab_sc[:].bitcast(I32), 0)
+                for quad in range(4):
+                    nc.sync.dma_start(
+                        tab_sc[32 * quad : 32 * quad + 8, :].bitcast(I32),
+                        tab_scales[:, 4 * quad : 4 * quad + 4, :].bitcast(I32),
+                    )
+
+        def load_wgs(queue, tile, ts):
+            dealt = wgs.rearrange("(q t) j -> q t j", t=4)[:, ts, :]
+            for quad in range(4):
+                queue.dma_start(tile[32 * quad : 32 * (quad + 1), :, :], dealt)
+
+        nc.vector.memset(warm[:, 0:1], 1.0)
+        nc.scalar.activation(warm[:, 1:2], warm[:, 0:1], ACT.Sqrt)
+
+        def load_weight(name, matrix, a, cols, offset):
+            raw = place(name, [P, 4, 512], F32, offset)
+            nc.sync.dma_start(raw[:], rows_4p_t(matrix, a)[:, :, cols])
+            return raw
+
+        w1_raw = {}
+        for a in range(2):
+            w1_raw[0, a] = load_weight(f"w1_raw0{a}", w1, a, slice(0, 512), W1_FIRST + a * 8 * KB)
+        nc.sync.dma_start(lift_sb[:], lift.rearrange("(g p t) -> p g t", g=2, t=4))
+        nc.sync.dma_start(idx2[:], offs2)
+
+        pages = {}
+        page_at = [PAGES + i * 8 * KB for i in range(4)] + [HS + i * 8 * KB for i in range(4)]
+        h_at = [HS + n * 4 * KB for n in (0, 2, 1, 3, 4, 6, 8, 9)]
+
+        def load_page(i):
+            g, t = divmod(i, 4)
+            page = place(f"page{i}", [P, T2], F32, page_at[i])
+            nc.sync.dma_start(page[:], rows_4p_t(page0, g)[:, t, :])
+            pages[i] = page
+
+        load_page(0)
+        nc.sync.dma_start(idx3[:], offs3)
+        load_page(1)
+        wgs_second = place("wgs_second", [P, 1, S], F32, WGS_SECOND)
+        load_wgs(nc.sync, wgs_second, slice(1, 2))
+        for a in range(2):
+            w1_raw[1, a] = load_weight(f"w1_raw1{a}", w1, a, slice(512, 1024), W1_SECOND + a * 8 * KB)
+        w2_raw = [load_weight(f"w2_raw{a}", w2, a, slice(0, N), W2_RAW + a * 8 * KB) for a in range(2)]
+        load_page(2)
+
+        nc.sync.dma_start(ease_sb[:], ease.rearrange("(g p t) -> p g t", g=2, t=4))
+        nc.sync.dma_start(tgain_sb[:], tgain.rearrange("(g p t) -> p g t", g=2, t=4))
+        wm = place("wm", [P, 2, 2 * N], U8, WM)
+        wm_sc = place("wm_sc", [P, 2, N], U8, WM + 2 * KB)
+        nc.vector.memset(wm_sc[:].bitcast(I32), 0)
+        for quad in range(4):
+            nc.sync.dma_start(
+                wm_sc[32 * quad : 32 * quad + 4, :, :].bitcast(I32),
+                wm_scales[:, 4 * quad : 4 * quad + 4, :].rearrange("a r c -> r a c").bitcast(I32),
+            )
+
+        picked = []
+        picked_sc = place("picked_sc", [P, S], U8, PICKED + 8 * KB)
+        for a in range(2):
+            words = place(f"picked{a}", [P, S], U32, PICKED + a * 4 * KB)
+            nc.vector.tensor_copy(words[:], tab[a][:].bitcast(U32).indirect(idx[:]))
+            picked.append(words)
+            if a == 0:
+                nc.vector.tensor_copy(picked_sc[:], tab_sc[:].indirect(idx[:]))
+        wgs_first = place("wgs_first", [P, 1, S], F32, TAB_SCALES)
+        load_wgs(nc.scalar, wgs_first, slice(0, 1))
+
+        def quantize(name, woven, words_at, scales_at):
+            width = woven.shape[1] // 4
+            words = place(name + "_words", [P, width], I32, words_at)
+            scales = place(name + "_scales", [P, width], U8, scales_at)
+            nc.vector.quantize_mx(words[:].bitcast(FP8X4), scales[:], woven[:])
+            return words, scales
+
+        def weave_w1(copy, g, a):
+            woven = place(f"w1_woven{g}{a}", [P, 2048], BF16, STAGING + a * 4 * KB)
+            copy(
+                woven[:].rearrange("p (t m j) -> p m j t", t=4, j=4),
+                w1_raw[g, a][:].rearrange("p j (m t) -> p m j t", t=4),
+            )
+            return woven
+
+        def weave4(copy, woven, rows):
+            copy(
+                woven.rearrange("p (c i t) -> p c t i", i=4, t=4)[:, :, 0 : rows.shape[1], :],
+                rows.rearrange("p t (c i) -> p c t i", i=4),
+            )
+
+        w1q = {}
+        for a in range(2):
+            woven = weave_w1(nc.vector.tensor_copy, 0, a)
+            w1q[0, a] = quantize(f"w1q0{a}", woven, W1_CODES + a * 2 * KB, W1_CODES + 8 * KB + a * 512)
+
+        wgs_rest = place("wgs_rest", [P, 2, S], F32, W1_FIRST)
+        load_wgs(nc.gpsimd, wgs_rest, slice(2, 4))
+        gains = [wgs_first[:, 0, :], wgs_second[:, 0, :], wgs_rest[:, 0, :], wgs_rest[:, 1, :]]
+
+        banks = [psum.tile([P, BANK], F32, name=f"strip{b}") for b in range(4)]
+        accs = [psum.tile([P, PM], F32, name=f"acc{b}") for b in range(4)]
+        hs = {}
+        mag_at = {2: W1_SECOND + 8 * KB, 3: W1_SECOND + 8 * KB, 4: W2_RAW + 8 * KB, 7: WOVEN + 6 * KB}
+        bent_at = 4 * [WOVEN + 6 * KB] + 3 * [TAB] + [W1_SECOND]
+
+        def make_h(i):
+            g, t = divmod(i, 4)
+            mag = place(f"mag{i}", [P, S], F32, mag_at.get(i, ABS + (i % 2) * 4 * KB))
+            h = place(f"h{i}", [P, S], F32, h_at[i])
+            for half in range(2):
+                cols = slice(half * BANK, (half + 1) * BANK)
+                bank = banks[2 * (i % 2) + half]
+                for a in range(2):
+                    words, scales = w1q[g, a]
+                    nc.tensor.matmul_mx(
+                        bank[:],
+                        lhsT=words[:, t * P : (t + 1) * P].bitcast(FP8X4),
+                        lhsT_scale=scales[:, t * P : (t + 1) * P],
+                        rhs=picked[a][:, cols].bitcast(FP8X4),
+                        rhs_scale=picked_sc[4 * a :, cols],
+                        start=(a == 0),
+                        stop=(a == 1),
+                    )
+                nc.scalar.activation(mag[:, cols], bank[:], ACT.Abs)
+                if i == 0:
+                    nc.scalar.activation(h[:, cols], mag[:, cols], ACT.Sqrt, bias=lift_sb[:, g, t : t + 1])
+            if i > 0:
+                nc.scalar.activation(h[:], mag[:], ACT.Sqrt, bias=lift_sb[:, g, t : t + 1])
+            hs[i] = h
+
+        for i in range(2):
+            make_h(i)
+
+        load_page(3)
+        nc.sync.dma_start(wm[:].bitcast(I32), wm_words.rearrange("a p c -> p a c").bitcast(I32))
+        w1_woven = [weave_w1(nc.scalar.copy, 1, a) for a in range(2)]
+        for i in range(2, 4):
+            make_h(i)
+        moons = [load_weight("moon0", moon, 0, slice(0, PM), MOON_FIRST)]
+
+        xs = {}
+        regrouped = {}
+
+        def scatter_and_fetch(i):
+            g, t = divmod(i, 4)
+            page = pages[i]
+            gain = gains[t]
+            if i == 0:
+                for half in range(2):
+                    cols = slice(half * BANK, (half + 1) * BANK)
+                    nc.vector.tensor_tensor(
+                        page[:].indirect(idx2[:, 32 * half : 32 * (half + 1)]), hs[i][:, cols], gain[:, cols], ALU.mult
+                    )
+            else:
+                nc.vector.tensor_tensor(page[:].indirect(idx2[:]), hs[i][:], gain, ALU.mult)
+            if 2 <= i < 6:
+                load_page(i + 2)
+            if t == 0:
+                xs[g] = place(f"x{g}", [P, 4, PM], F32, X_FIRST if g == 0 else W2_RAW)
+            nc.vector.tensor_copy(xs[g][:, t, :], page[:].indirect(idx3[:]))
+            if i == 0:
+                regrouped[0] = place("regrouped0", [P, 4, T2], F32, TAB)
+            if i == 4:
+                regrouped[1] = place("regrouped1", [P, 3, T2], F32, W1_FIRST + 8 * KB)
+            if i < 7:
+                (nc.gpsimd if g == 0 else nc.sync).dma_start(regrouped[g][:, t, :], page[:])
+            if i > 5:
+                nc.sync.dma_start(rows_4p_t(out_1, g)[:, t, :], page[:])
+            if i == 3:
+                moons.append(load_weight("moon1", moon, 1, slice(0, PM), page_at[3]))
+                nc.gpsimd.dma_start(rows_4p_t(out_1, g), regrouped[g][:])
+            if i == 5:
+                nc.sync.dma_start(rows_4p_t(out_1, g)[:, 0:2, :], regrouped[g][:, 0:2, :])
+
+        arcs = {}
+
+        def make_arc(i):
+            g, t = divmod(i, 4)
+            if t == 0:
+                arcs[g] = place(f"arc{g}", [P, PM * 4], BF16, STAGING if g == 0 else PICKED)
+            bent = place(f"bent{i}", [P, PM], F32, bent_at[i])
+            nc.scalar.activation(bent[:], xs[g][:, t, :], ACT.Tanh, scale=ease_sb[:, g, t : t + 1])
+            nc.scalar.activation(
+                arcs[g][:].rearrange("p (m t) -> p m t", t=4)[:, :, t], bent[:], ACT.Copy,
+                scale=tgain_sb[:, g, t : t + 1],
+            )
+
+        def make_lit(g):
+            lit = place(f"lit{g}", [P, PM * 4], BF16, (STAGING if g == 0 else PICKED) + 4 * KB)
+            nc.vector.tensor_tensor(
+                lit[:].rearrange("p (c i t) -> p c t i", i=4, t=4),
+                xs[g][:].rearrange("p t (c i) -> p c t i", i=4),
+                moons[g][:].rearrange("p t (c i) -> p c t i", i=4),
+                ALU.add,
+            )
+            return lit
+
+        def moon_passes(g, litq):
+            for nt in range(4):
+                nc.tensor.matmul_mx(
+                    accs[nt][:],
+                    lhsT=wm[:, g, 2 * P * nt : 2 * P * (nt + 1)].bitcast(FP4X4),
+                    lhsT_scale=wm_sc[:, g, P * nt : P * (nt + 1)],
+                    rhs=litq[0][:].bitcast(FP8X4),
+                    rhs_scale=litq[1][:],
+                    start=(g == 0),
+                    stop=False,
+                )
+
+        def arc_pass(g, nt, arcq):
+            words, scales = w2q[g]
+            nc.tensor.matmul_mx(
+                accs[nt][:],
+                lhsT=words[:, P * nt : P * (nt + 1)].bitcast(FP8X4),
+                lhsT_scale=scales[:, P * nt : P * (nt + 1)],
+                rhs=arcq[0][:].bitcast(FP8X4),
+                rhs_scale=arcq[1][:],
+                start=False,
+                stop=(g == 1),
+            )
+
+        def quantize_page_chunk(g, c, woven, scales, words_at):
+            words = place(f"page_words{g}{c}", [P, CHUNK], I32, words_at)
+            cols = slice(c * CHUNK, (c + 1) * CHUNK)
+            nc.vector.quantize_mx(words[:].bitcast(FP8X4), scales[:, cols], woven)
+            nc.sync.dma_start(out_2[g][:, cols, :].rearrange("p m t -> p (m t)").bitcast(I32), words[:])
+
+        def weave_page(g, offset):
+            woven = place(f"woven_page{g}", [P, 4 * T2], BF16, offset)
+            chunks = [woven[:, 4 * c * CHUNK : 4 * (c + 1) * CHUNK] for c in range(CHUNKS)]
+            for c in range(CHUNKS):
+                weave4(nc.scalar.copy, chunks[c], regrouped[g][:, :, c * CHUNK : (c + 1) * CHUNK])
+            return chunks
+
+        def store_page_scales(g, scales):
+            for quad in range(4):
+                nc.sync.dma_start(
+                    out_3[g][4 * quad : 4 * quad + 4, :].bitcast(I32),
+                    scales[32 * quad : 32 * quad + 4, :].bitcast(I32),
+                )
+
+        scatter_and_fetch(0)
+        scatter_and_fetch(1)
+        for a in range(2):
+            w1q[1, a] = quantize(
+                f"w1q1{a}", w1_woven[a], W1_CODES + (2 + a) * 2 * KB, h_at[1] + a * 512
+            )
+        w2_woven = []
+        for a in range(2):
+            woven = place(f"w2_woven{a}", [P, 4 * N], BF16, WOVEN + a * 12 * KB)
+            weave4(nc.scalar.copy, woven[:], w2_raw[a][:])
+            w2_woven.append(woven)
+        for i in range(4, 8):
+            make_h(i)
+        scatter_and_fetch(2)
+        w2q = [
+            quantize(f"w2q{a}", w2_woven[a], W2_CODES + a * 2 * KB, LATE_SCALES + 3 * KB + a * 512) for a in range(2)
+        ]
+        for i in range(3):
+            make_arc(i)
+        scatter_and_fetch(3)
+        lit = make_lit(0)
+        make_arc(3)
+        woven_page = weave_page(0, WOVEN)
+        scatter_and_fetch(4)
+        litq = quantize("litq0", lit, W1_CODES + 6 * KB, page_at[4])
+        arcq = quantize("arcq0", arcs[0], W2_RAW + 10 * KB, page_at[4] + 512)
+        moon_passes(0, litq)
+        for nt in range(4):
+            arc_pass(0, nt, arcq)
+        make_arc(4)
+        scatter_and_fetch(5)
+        page_scales = place("page_scales0", [P, T2], U8, page_at[5])
+        for c in range(CHUNKS):
+            quantize_page_chunk(0, c, woven_page[c], page_scales, page_at[0] + c * 2 * KB)
+        store_page_scales(0, page_scales)
+        make_arc(5)
+
+        def weave_one(i, c):
+            nc.scalar.copy(
+                woven_page[c].rearrange("p (m t) -> p m t", t=4)[:, :, i % 4],
+                pages[i][:, c * CHUNK : (c + 1) * CHUNK],
+            )
+
+        scatter_and_fetch(6)
+        make_arc(6)
+        woven_page = weave_page(1, TAB)
+        scatter_and_fetch(7)
+        weave_one(7, 0)
+        lit = make_lit(1)
+        make_arc(7)
+        litq = quantize("litq1", lit, W2_RAW + 12 * KB, LATE_SCALES + 2 * KB)
+        moon_passes(1, litq)
+        page_scales = place("page_scales1", [P, T2], U8, LATE_SCALES)
+        quantize_page_chunk(1, 0, woven_page[0], page_scales, page_at[1])
+        arcq = quantize("arcq1", arcs[1], W2_RAW + 14 * KB, LATE_SCALES + 2 * KB + 512)
+        for nt in range(4):
+            arc_pass(1, nt, arcq)
+        for c in range(1, CHUNKS):
+            weave_one(7, c)
+        for nt in range(4):
+            if nt > 0:
+                quantize_page_chunk(1, nt, woven_page[nt], page_scales, page_at[1] + nt * 2 * KB)
+            y = place(f"y{nt}", [P, PM], F32, page_at[2] + nt * 2 * KB)
+            nc.vector.tensor_copy(y[:], accs[nt][:])
+            nc.sync.dma_start(out_0[P * nt : P * (nt + 1), :], y[:])
+        store_page_scales(1, page_scales)

@@ -17,14 +17,22 @@ ACT = mybir.ActivationFunctionType
 ALU = mybir.AluOpType
 
 P = 128
-KB = 1024
+PACK = 4
+PASS = P * PACK
+GROUPS = H // PASS
+TILES = GROUPS * PACK
+QUADS = 4
 BANK = 512
 CHUNK = 512
 CHUNKS = T2 // CHUNK
+N_TILES = N // P
+AHEAD = 2
 
+KB = 1024
 TAB = 0
 W1_FIRST = 32 * KB
 W1_SECOND = 48 * KB
+REGROUPED_SECOND = W1_FIRST + 8 * KB
 PAGES = 64 * KB
 WGS_SECOND = 96 * KB
 LATE_SCALES = 100 * KB
@@ -41,6 +49,20 @@ X_FIRST = 214 * KB
 ABS = 222 * KB
 MOON_FIRST = 230 * KB
 
+ROWS_BYTES = 8 * KB
+H_BYTES = 4 * KB
+WORDS_BYTES = 2 * KB
+PLANE_BYTES = 512
+
+PAGE_AT = [PAGES + i * ROWS_BYTES for i in range(PACK)] + [HS + i * ROWS_BYTES for i in range(PACK)]
+H_AT = [HS + slot * H_BYTES for slot in (0, 2, 1, 3, 4, 6, 8, 9)]
+FIRST_TANH_AT = WOVEN + 6 * KB
+MAG_AT = [
+    ABS, ABS + H_BYTES, W1_SECOND + ROWS_BYTES, W1_SECOND + ROWS_BYTES,
+    W2_RAW + ROWS_BYTES, ABS + H_BYTES, ABS, FIRST_TANH_AT,
+]
+TANH_AT = 4 * [FIRST_TANH_AT] + 3 * [TAB] + [W1_SECOND]
+
 
 def tile_list_auroral_arc_page_kernel(
     tc, tab_words, tab_scales, offs, w1, lift, page0, wgs, offs2, offs3, ease, tgain, moon, w2,
@@ -56,85 +78,96 @@ def tile_list_auroral_arc_page_kernel(
             return sb.tile(shape, dtype, name=name, offset=offset, align_bytes=64)
 
         def rows_4p_t(matrix, g):
-            return matrix[512 * g : 512 * (g + 1), :].rearrange("(p t) c -> p t c", t=4)
+            return matrix[PASS * g : PASS * (g + 1), :].rearrange("(p t) c -> p t c", t=PACK)
+
+        def load_rows(name, matrix, g, cols, offset):
+            raw = place(name, [P, PACK, 512], F32, offset)
+            nc.sync.dma_start(raw[:], rows_4p_t(matrix, g)[:, :, cols])
+            return raw
+
+        def load_per_row(tile, vector):
+            nc.sync.dma_start(tile[:], vector.rearrange("(g p t) -> p g t", g=GROUPS, t=PACK))
+
+        def load_wgs(queue, tile, ts):
+            dealt = wgs.rearrange("(q t) j -> q t j", t=PACK)[:, ts, :]
+            for quad in range(QUADS):
+                queue.dma_start(tile[32 * quad : 32 * (quad + 1), :, :], dealt)
+
+        pages = {}
+
+        def load_page(i):
+            g, t = divmod(i, PACK)
+            pages[i] = place(f"page{i}", [P, T2], F32, PAGE_AT[i])
+            nc.sync.dma_start(pages[i][:], rows_4p_t(page0, g)[:, t, :])
+
+        def quantize(name, woven, words_at, scales_at):
+            width = woven.shape[1] // PACK
+            words = place(name + "_words", [P, width], I32, words_at)
+            scales = place(name + "_scales", [P, width], U8, scales_at)
+            nc.vector.quantize_mx(words[:].bitcast(FP8X4), scales[:], woven[:])
+            return words, scales
+
+        def by_four_columns(rows):
+            return rows.rearrange("p t (c i) -> p c t i", i=4)
+
+        def woven_by_four_columns(woven):
+            return woven.rearrange("p (c i t) -> p c t i", i=4, t=PACK)
+
+        def weave(woven, rows):
+            nc.scalar.copy(woven_by_four_columns(woven)[:, :, 0 : rows.shape[1], :], by_four_columns(rows))
 
         idx = lists.tile([P, S // 16], U16, name="idx")
         idx2 = lists.tile([P, S // 16], U16, name="idx2")
         idx3 = lists.tile([P, PM // 16], U16, name="idx3")
-        lift_sb = lists.tile([P, 2, 4], F32, name="lift_sb")
-        ease_sb = lists.tile([P, 2, 4], F32, name="ease_sb")
-        tgain_sb = lists.tile([P, 2, 4], F32, name="tgain_sb")
-        warm = lists.tile([P, 2], F32, name="warm")
+        lift_sb = lists.tile([P, GROUPS, PACK], F32, name="lift_sb")
+        ease_sb = lists.tile([P, GROUPS, PACK], F32, name="ease_sb")
+        tgain_sb = lists.tile([P, GROUPS, PACK], F32, name="tgain_sb")
 
         nc.sync.dma_start(idx[:], offs)
         tab = []
-        for a in range(2):
-            words = place(f"tab{a}", [P, T], I32, TAB + a * 16 * KB)
+        for a in range(GROUPS):
+            words = place(f"tab{a}", [P, T], I32, TAB + a * 4 * T)
             nc.sync.dma_start(words[:], tab_words[a].rearrange("p c i -> p (c i)").bitcast(I32))
             tab.append(words)
             if a == 0:
                 tab_sc = place("tab_sc", [P, T], U8, TAB_SCALES)
                 nc.vector.memset(tab_sc[:].bitcast(I32), 0)
-                for quad in range(4):
+                for quad in range(QUADS):
                     nc.sync.dma_start(
                         tab_sc[32 * quad : 32 * quad + 8, :].bitcast(I32),
                         tab_scales[:, 4 * quad : 4 * quad + 4, :].bitcast(I32),
                     )
 
-        def load_wgs(queue, tile, ts):
-            dealt = wgs.rearrange("(q t) j -> q t j", t=4)[:, ts, :]
-            for quad in range(4):
-                queue.dma_start(tile[32 * quad : 32 * (quad + 1), :, :], dealt)
-
-        nc.vector.memset(warm[:, 0:1], 1.0)
-        nc.scalar.activation(warm[:, 1:2], warm[:, 0:1], ACT.Sqrt)
-
-        def load_weight(name, matrix, a, cols, offset):
-            raw = place(name, [P, 4, 512], F32, offset)
-            nc.sync.dma_start(raw[:], rows_4p_t(matrix, a)[:, :, cols])
-            return raw
-
         w1_raw = {}
-        for a in range(2):
-            w1_raw[0, a] = load_weight(f"w1_raw0{a}", w1, a, slice(0, 512), W1_FIRST + a * 8 * KB)
-        nc.sync.dma_start(lift_sb[:], lift.rearrange("(g p t) -> p g t", g=2, t=4))
+        for a in range(GROUPS):
+            w1_raw[0, a] = load_rows(f"w1_raw0{a}", w1, a, slice(0, PASS), W1_FIRST + a * ROWS_BYTES)
+        load_per_row(lift_sb, lift)
         nc.sync.dma_start(idx2[:], offs2)
-
-        pages = {}
-        page_at = [PAGES + i * 8 * KB for i in range(4)] + [HS + i * 8 * KB for i in range(4)]
-        h_at = [HS + n * 4 * KB for n in (0, 2, 1, 3, 4, 6, 8, 9)]
-
-        def load_page(i):
-            g, t = divmod(i, 4)
-            page = place(f"page{i}", [P, T2], F32, page_at[i])
-            nc.sync.dma_start(page[:], rows_4p_t(page0, g)[:, t, :])
-            pages[i] = page
-
         load_page(0)
         nc.sync.dma_start(idx3[:], offs3)
         load_page(1)
         wgs_second = place("wgs_second", [P, 1, S], F32, WGS_SECOND)
         load_wgs(nc.sync, wgs_second, slice(1, 2))
-        for a in range(2):
-            w1_raw[1, a] = load_weight(f"w1_raw1{a}", w1, a, slice(512, 1024), W1_SECOND + a * 8 * KB)
-        w2_raw = [load_weight(f"w2_raw{a}", w2, a, slice(0, N), W2_RAW + a * 8 * KB) for a in range(2)]
+        for a in range(GROUPS):
+            w1_raw[1, a] = load_rows(f"w1_raw1{a}", w1, a, slice(PASS, H), W1_SECOND + a * ROWS_BYTES)
+        w2_raw = [load_rows(f"w2_raw{g}", w2, g, slice(0, N), W2_RAW + g * ROWS_BYTES) for g in range(GROUPS)]
         load_page(2)
+        load_per_row(ease_sb, ease)
+        load_per_row(tgain_sb, tgain)
 
-        nc.sync.dma_start(ease_sb[:], ease.rearrange("(g p t) -> p g t", g=2, t=4))
-        nc.sync.dma_start(tgain_sb[:], tgain.rearrange("(g p t) -> p g t", g=2, t=4))
-        wm = place("wm", [P, 2, 2 * N], U8, WM)
-        wm_sc = place("wm_sc", [P, 2, N], U8, WM + 2 * KB)
+        wm = place("wm", [P, GROUPS, 2 * N], U8, WM)
+        wm_sc = place("wm_sc", [P, GROUPS, N], U8, WM + GROUPS * 2 * N)
         nc.vector.memset(wm_sc[:].bitcast(I32), 0)
-        for quad in range(4):
+        for quad in range(QUADS):
             nc.sync.dma_start(
                 wm_sc[32 * quad : 32 * quad + 4, :, :].bitcast(I32),
                 wm_scales[:, 4 * quad : 4 * quad + 4, :].rearrange("a r c -> r a c").bitcast(I32),
             )
 
         picked = []
-        picked_sc = place("picked_sc", [P, S], U8, PICKED + 8 * KB)
-        for a in range(2):
-            words = place(f"picked{a}", [P, S], U32, PICKED + a * 4 * KB)
+        picked_sc = place("picked_sc", [P, S], U8, PICKED + GROUPS * H_BYTES)
+        for a in range(GROUPS):
+            words = place(f"picked{a}", [P, S], U32, PICKED + a * H_BYTES)
             nc.vector.tensor_copy(words[:], tab[a][:].bitcast(U32).indirect(idx[:]))
             picked.append(words)
             if a == 0:
@@ -142,50 +175,38 @@ def tile_list_auroral_arc_page_kernel(
         wgs_first = place("wgs_first", [P, 1, S], F32, TAB_SCALES)
         load_wgs(nc.scalar, wgs_first, slice(0, 1))
 
-        def quantize(name, woven, words_at, scales_at):
-            width = woven.shape[1] // 4
-            words = place(name + "_words", [P, width], I32, words_at)
-            scales = place(name + "_scales", [P, width], U8, scales_at)
-            nc.vector.quantize_mx(words[:].bitcast(FP8X4), scales[:], woven[:])
-            return words, scales
-
         def weave_w1(copy, g, a):
-            woven = place(f"w1_woven{g}{a}", [P, 2048], BF16, STAGING + a * 4 * KB)
+            woven = place(f"w1_woven{g}{a}", [P, PACK * PASS], BF16, STAGING + a * H_BYTES)
             copy(
-                woven[:].rearrange("p (t m j) -> p m j t", t=4, j=4),
-                w1_raw[g, a][:].rearrange("p j (m t) -> p m j t", t=4),
+                woven[:].rearrange("p (t m j) -> p m j t", t=PACK, j=PACK),
+                w1_raw[g, a][:].rearrange("p j (m t) -> p m j t", t=PACK),
             )
             return woven
 
-        def weave4(copy, woven, rows):
-            copy(
-                woven.rearrange("p (c i t) -> p c t i", i=4, t=4)[:, :, 0 : rows.shape[1], :],
-                rows.rearrange("p t (c i) -> p c t i", i=4),
-            )
-
         w1q = {}
-        for a in range(2):
+        for a in range(GROUPS):
             woven = weave_w1(nc.vector.tensor_copy, 0, a)
-            w1q[0, a] = quantize(f"w1q0{a}", woven, W1_CODES + a * 2 * KB, W1_CODES + 8 * KB + a * 512)
+            w1q[0, a] = quantize(
+                f"w1q0{a}", woven, W1_CODES + a * WORDS_BYTES, W1_CODES + 4 * WORDS_BYTES + a * PLANE_BYTES
+            )
 
         wgs_rest = place("wgs_rest", [P, 2, S], F32, W1_FIRST)
         load_wgs(nc.gpsimd, wgs_rest, slice(2, 4))
         gains = [wgs_first[:, 0, :], wgs_second[:, 0, :], wgs_rest[:, 0, :], wgs_rest[:, 1, :]]
 
         banks = [psum.tile([P, BANK], F32, name=f"strip{b}") for b in range(4)]
-        accs = [psum.tile([P, PM], F32, name=f"acc{b}") for b in range(4)]
+        accs = [psum.tile([P, PM], F32, name=f"acc{nt}") for nt in range(N_TILES)]
+        halves = [slice(half * BANK, (half + 1) * BANK) for half in range(S // BANK)]
         hs = {}
-        mag_at = {2: W1_SECOND + 8 * KB, 3: W1_SECOND + 8 * KB, 4: W2_RAW + 8 * KB, 7: WOVEN + 6 * KB}
-        bent_at = 4 * [WOVEN + 6 * KB] + 3 * [TAB] + [W1_SECOND]
 
         def make_h(i):
-            g, t = divmod(i, 4)
-            mag = place(f"mag{i}", [P, S], F32, mag_at.get(i, ABS + (i % 2) * 4 * KB))
-            h = place(f"h{i}", [P, S], F32, h_at[i])
-            for half in range(2):
-                cols = slice(half * BANK, (half + 1) * BANK)
+            g, t = divmod(i, PACK)
+            mag = place(f"mag{i}", [P, S], F32, MAG_AT[i])
+            hs[i] = place(f"h{i}", [P, S], F32, H_AT[i])
+            row_lift = lift_sb[:, g, t : t + 1]
+            for half, cols in enumerate(halves):
                 bank = banks[2 * (i % 2) + half]
-                for a in range(2):
+                for a in range(GROUPS):
                     words, scales = w1q[g, a]
                     nc.tensor.matmul_mx(
                         bank[:],
@@ -194,84 +215,73 @@ def tile_list_auroral_arc_page_kernel(
                         rhs=picked[a][:, cols].bitcast(FP8X4),
                         rhs_scale=picked_sc[4 * a :, cols],
                         start=(a == 0),
-                        stop=(a == 1),
+                        stop=(a == GROUPS - 1),
                     )
                 nc.scalar.activation(mag[:, cols], bank[:], ACT.Abs)
                 if i == 0:
-                    nc.scalar.activation(h[:, cols], mag[:, cols], ACT.Sqrt, bias=lift_sb[:, g, t : t + 1])
+                    nc.scalar.activation(hs[i][:, cols], mag[:, cols], ACT.Sqrt, bias=row_lift)
             if i > 0:
-                nc.scalar.activation(h[:], mag[:], ACT.Sqrt, bias=lift_sb[:, g, t : t + 1])
-            hs[i] = h
+                nc.scalar.activation(hs[i][:], mag[:], ACT.Sqrt, bias=row_lift)
 
-        for i in range(2):
-            make_h(i)
-
+        make_h(0)
+        make_h(1)
         load_page(3)
         nc.sync.dma_start(wm[:].bitcast(I32), wm_words.rearrange("a p c -> p a c").bitcast(I32))
-        w1_woven = [weave_w1(nc.scalar.copy, 1, a) for a in range(2)]
-        for i in range(2, 4):
-            make_h(i)
-        moons = [load_weight("moon0", moon, 0, slice(0, PM), MOON_FIRST)]
+        w1_woven = [weave_w1(nc.scalar.copy, 1, a) for a in range(GROUPS)]
+        make_h(2)
+        make_h(3)
+        moons = [load_rows("moon0", moon, 0, slice(0, PM), MOON_FIRST)]
 
         xs = {}
-        regrouped = {}
 
         def scatter_and_fetch(i):
-            g, t = divmod(i, 4)
+            g, t = divmod(i, PACK)
             page = pages[i]
-            gain = gains[t]
             if i == 0:
-                for half in range(2):
-                    cols = slice(half * BANK, (half + 1) * BANK)
-                    nc.vector.tensor_tensor(
-                        page[:].indirect(idx2[:, 32 * half : 32 * (half + 1)]), hs[i][:, cols], gain[:, cols], ALU.mult
-                    )
+                for cols in halves:
+                    entries = idx2[:, cols.start // 16 : cols.stop // 16]
+                    nc.vector.tensor_tensor(page[:].indirect(entries), hs[i][:, cols], gains[t][:, cols], ALU.mult)
             else:
-                nc.vector.tensor_tensor(page[:].indirect(idx2[:]), hs[i][:], gain, ALU.mult)
-            if 2 <= i < 6:
-                load_page(i + 2)
+                nc.vector.tensor_tensor(page[:].indirect(idx2[:]), hs[i][:], gains[t], ALU.mult)
+            if AHEAD <= i < TILES - AHEAD:
+                load_page(i + AHEAD)
             if t == 0:
-                xs[g] = place(f"x{g}", [P, 4, PM], F32, X_FIRST if g == 0 else W2_RAW)
+                xs[g] = place(f"x{g}", [P, PACK, PM], F32, X_FIRST if g == 0 else W2_RAW)
             nc.vector.tensor_copy(xs[g][:, t, :], page[:].indirect(idx3[:]))
-            if i == 0:
-                regrouped[0] = place("regrouped0", [P, 4, T2], F32, TAB)
-            if i == 4:
-                regrouped[1] = place("regrouped1", [P, 3, T2], F32, W1_FIRST + 8 * KB)
-            if i < 7:
-                (nc.gpsimd if g == 0 else nc.sync).dma_start(regrouped[g][:, t, :], page[:])
-            if i > 5:
-                nc.sync.dma_start(rows_4p_t(out_1, g)[:, t, :], page[:])
-            if i == 3:
-                moons.append(load_weight("moon1", moon, 1, slice(0, PM), page_at[3]))
-                nc.gpsimd.dma_start(rows_4p_t(out_1, g), regrouped[g][:])
-            if i == 5:
-                nc.sync.dma_start(rows_4p_t(out_1, g)[:, 0:2, :], regrouped[g][:, 0:2, :])
+
+        regrouped = {}
+
+        def regroup(i):
+            g, t = divmod(i, PACK)
+            queue = nc.gpsimd if g == 0 else nc.sync
+            queue.dma_start(regrouped[g][:, t, :], pages[i][:])
+
+        def store_page(i):
+            g, t = divmod(i, PACK)
+            nc.sync.dma_start(rows_4p_t(out_1, g)[:, t, :], pages[i][:])
 
         arcs = {}
 
         def make_arc(i):
-            g, t = divmod(i, 4)
+            g, t = divmod(i, PACK)
             if t == 0:
-                arcs[g] = place(f"arc{g}", [P, PM * 4], BF16, STAGING if g == 0 else PICKED)
-            bent = place(f"bent{i}", [P, PM], F32, bent_at[i])
+                arcs[g] = place(f"arc{g}", [P, PM * PACK], BF16, STAGING if g == 0 else PICKED)
+            bent = place(f"bent{i}", [P, PM], F32, TANH_AT[i])
             nc.scalar.activation(bent[:], xs[g][:, t, :], ACT.Tanh, scale=ease_sb[:, g, t : t + 1])
             nc.scalar.activation(
-                arcs[g][:].rearrange("p (m t) -> p m t", t=4)[:, :, t], bent[:], ACT.Copy,
+                arcs[g][:].rearrange("p (m t) -> p m t", t=PACK)[:, :, t], bent[:], ACT.Copy,
                 scale=tgain_sb[:, g, t : t + 1],
             )
 
         def make_lit(g):
-            lit = place(f"lit{g}", [P, PM * 4], BF16, (STAGING if g == 0 else PICKED) + 4 * KB)
+            lit = place(f"lit{g}", [P, PM * PACK], BF16, (STAGING if g == 0 else PICKED) + H_BYTES)
             nc.vector.tensor_tensor(
-                lit[:].rearrange("p (c i t) -> p c t i", i=4, t=4),
-                xs[g][:].rearrange("p t (c i) -> p c t i", i=4),
-                moons[g][:].rearrange("p t (c i) -> p c t i", i=4),
-                ALU.add,
+                woven_by_four_columns(lit[:]), by_four_columns(xs[g][:]), by_four_columns(moons[g][:]), ALU.add
             )
             return lit
 
         def moon_passes(g, litq):
-            for nt in range(4):
+            for nt in range(N_TILES):
                 nc.tensor.matmul_mx(
                     accs[nt][:],
                     lhsT=wm[:, g, 2 * P * nt : 2 * P * (nt + 1)].bitcast(FP4X4),
@@ -282,101 +292,116 @@ def tile_list_auroral_arc_page_kernel(
                     stop=False,
                 )
 
-        def arc_pass(g, nt, arcq):
+        def arc_passes(g, arcq):
             words, scales = w2q[g]
-            nc.tensor.matmul_mx(
-                accs[nt][:],
-                lhsT=words[:, P * nt : P * (nt + 1)].bitcast(FP8X4),
-                lhsT_scale=scales[:, P * nt : P * (nt + 1)],
-                rhs=arcq[0][:].bitcast(FP8X4),
-                rhs_scale=arcq[1][:],
-                start=False,
-                stop=(g == 1),
-            )
-
-        def quantize_page_chunk(g, c, woven, scales, words_at):
-            words = place(f"page_words{g}{c}", [P, CHUNK], I32, words_at)
-            cols = slice(c * CHUNK, (c + 1) * CHUNK)
-            nc.vector.quantize_mx(words[:].bitcast(FP8X4), scales[:, cols], woven)
-            nc.sync.dma_start(out_2[g][:, cols, :].rearrange("p m t -> p (m t)").bitcast(I32), words[:])
+            for nt in range(N_TILES):
+                nc.tensor.matmul_mx(
+                    accs[nt][:],
+                    lhsT=words[:, P * nt : P * (nt + 1)].bitcast(FP8X4),
+                    lhsT_scale=scales[:, P * nt : P * (nt + 1)],
+                    rhs=arcq[0][:].bitcast(FP8X4),
+                    rhs_scale=arcq[1][:],
+                    start=False,
+                    stop=(g == GROUPS - 1),
+                )
 
         def weave_page(g, offset):
-            woven = place(f"woven_page{g}", [P, 4 * T2], BF16, offset)
-            chunks = [woven[:, 4 * c * CHUNK : 4 * (c + 1) * CHUNK] for c in range(CHUNKS)]
+            woven = place(f"woven_page{g}", [P, PACK * T2], BF16, offset)
+            chunks = [woven[:, PACK * c * CHUNK : PACK * (c + 1) * CHUNK] for c in range(CHUNKS)]
             for c in range(CHUNKS):
-                weave4(nc.scalar.copy, chunks[c], regrouped[g][:, :, c * CHUNK : (c + 1) * CHUNK])
+                weave(chunks[c], regrouped[g][:, :, c * CHUNK : (c + 1) * CHUNK])
             return chunks
 
+        def weave_last_tile(chunks, c):
+            nc.scalar.copy(
+                chunks[c].rearrange("p (m t) -> p m t", t=PACK)[:, :, PACK - 1],
+                pages[TILES - 1][:, c * CHUNK : (c + 1) * CHUNK],
+            )
+
+        def quantize_page_chunk(g, c, chunks, scales, words_at):
+            words = place(f"page_words{g}{c}", [P, CHUNK], I32, words_at + c * WORDS_BYTES)
+            cols = slice(c * CHUNK, (c + 1) * CHUNK)
+            nc.vector.quantize_mx(words[:].bitcast(FP8X4), scales[:, cols], chunks[c])
+            nc.sync.dma_start(out_2[g][:, cols, :].rearrange("p m t -> p (m t)").bitcast(I32), words[:])
+
         def store_page_scales(g, scales):
-            for quad in range(4):
+            for quad in range(QUADS):
                 nc.sync.dma_start(
                     out_3[g][4 * quad : 4 * quad + 4, :].bitcast(I32),
                     scales[32 * quad : 32 * quad + 4, :].bitcast(I32),
                 )
 
         scatter_and_fetch(0)
+        regrouped[0] = place("regrouped0", [P, PACK, T2], F32, TAB)
+        regroup(0)
         scatter_and_fetch(1)
-        for a in range(2):
+        regroup(1)
+        for a in range(GROUPS):
             w1q[1, a] = quantize(
-                f"w1q1{a}", w1_woven[a], W1_CODES + (2 + a) * 2 * KB, h_at[1] + a * 512
+                f"w1q1{a}", w1_woven[a], W1_CODES + (GROUPS + a) * WORDS_BYTES, H_AT[1] + a * PLANE_BYTES
             )
         w2_woven = []
-        for a in range(2):
-            woven = place(f"w2_woven{a}", [P, 4 * N], BF16, WOVEN + a * 12 * KB)
-            weave4(nc.scalar.copy, woven[:], w2_raw[a][:])
+        for g in range(GROUPS):
+            woven = place(f"w2_woven{g}", [P, PACK * N], BF16, WOVEN + g * 3 * H_BYTES)
+            weave(woven[:], w2_raw[g][:])
             w2_woven.append(woven)
-        for i in range(4, 8):
+        for i in range(PACK, TILES):
             make_h(i)
         scatter_and_fetch(2)
+        regroup(2)
         w2q = [
-            quantize(f"w2q{a}", w2_woven[a], W2_CODES + a * 2 * KB, LATE_SCALES + 3 * KB + a * 512) for a in range(2)
+            quantize(f"w2q{g}", w2_woven[g], W2_CODES + g * WORDS_BYTES, LATE_SCALES + 3 * KB + g * PLANE_BYTES)
+            for g in range(GROUPS)
         ]
         for i in range(3):
             make_arc(i)
         scatter_and_fetch(3)
+        regroup(3)
+        moons.append(load_rows("moon1", moon, 1, slice(0, PM), PAGE_AT[3]))
+        nc.gpsimd.dma_start(rows_4p_t(out_1, 0), regrouped[0][:])
         lit = make_lit(0)
         make_arc(3)
-        woven_page = weave_page(0, WOVEN)
+        chunks = weave_page(0, WOVEN)
+
         scatter_and_fetch(4)
-        litq = quantize("litq0", lit, W1_CODES + 6 * KB, page_at[4])
-        arcq = quantize("arcq0", arcs[0], W2_RAW + 10 * KB, page_at[4] + 512)
+        regrouped[1] = place("regrouped1", [P, PACK - 1, T2], F32, REGROUPED_SECOND)
+        regroup(4)
+        litq = quantize("litq0", lit, W1_CODES + 3 * WORDS_BYTES, PAGE_AT[4])
+        arcq = quantize("arcq0", arcs[0], W2_RAW + ROWS_BYTES + WORDS_BYTES, PAGE_AT[4] + PLANE_BYTES)
         moon_passes(0, litq)
-        for nt in range(4):
-            arc_pass(0, nt, arcq)
+        arc_passes(0, arcq)
         make_arc(4)
         scatter_and_fetch(5)
-        page_scales = place("page_scales0", [P, T2], U8, page_at[5])
+        regroup(5)
+        nc.sync.dma_start(rows_4p_t(out_1, 1)[:, 0:2, :], regrouped[1][:, 0:2, :])
+        page_scales = place("page_scales0", [P, T2], U8, PAGE_AT[5])
         for c in range(CHUNKS):
-            quantize_page_chunk(0, c, woven_page[c], page_scales, page_at[0] + c * 2 * KB)
+            quantize_page_chunk(0, c, chunks, page_scales, PAGE_AT[0])
         store_page_scales(0, page_scales)
         make_arc(5)
-
-        def weave_one(i, c):
-            nc.scalar.copy(
-                woven_page[c].rearrange("p (m t) -> p m t", t=4)[:, :, i % 4],
-                pages[i][:, c * CHUNK : (c + 1) * CHUNK],
-            )
-
         scatter_and_fetch(6)
+        regroup(6)
+        store_page(6)
         make_arc(6)
-        woven_page = weave_page(1, TAB)
+        chunks = weave_page(1, TAB)
         scatter_and_fetch(7)
-        weave_one(7, 0)
+        store_page(7)
+
+        weave_last_tile(chunks, 0)
         lit = make_lit(1)
         make_arc(7)
-        litq = quantize("litq1", lit, W2_RAW + 12 * KB, LATE_SCALES + 2 * KB)
+        litq = quantize("litq1", lit, W2_RAW + ROWS_BYTES + 2 * WORDS_BYTES, LATE_SCALES + T2)
         moon_passes(1, litq)
         page_scales = place("page_scales1", [P, T2], U8, LATE_SCALES)
-        quantize_page_chunk(1, 0, woven_page[0], page_scales, page_at[1])
-        arcq = quantize("arcq1", arcs[1], W2_RAW + 14 * KB, LATE_SCALES + 2 * KB + 512)
-        for nt in range(4):
-            arc_pass(1, nt, arcq)
+        quantize_page_chunk(1, 0, chunks, page_scales, PAGE_AT[1])
+        arcq = quantize("arcq1", arcs[1], W2_RAW + ROWS_BYTES + 3 * WORDS_BYTES, LATE_SCALES + T2 + PLANE_BYTES)
+        arc_passes(1, arcq)
         for c in range(1, CHUNKS):
-            weave_one(7, c)
-        for nt in range(4):
+            weave_last_tile(chunks, c)
+        for nt in range(N_TILES):
             if nt > 0:
-                quantize_page_chunk(1, nt, woven_page[nt], page_scales, page_at[1] + nt * 2 * KB)
-            y = place(f"y{nt}", [P, PM], F32, page_at[2] + nt * 2 * KB)
+                quantize_page_chunk(1, nt, chunks, page_scales, PAGE_AT[1])
+            y = place(f"y{nt}", [P, PM], F32, PAGE_AT[2] + nt * 4 * PM)
             nc.vector.tensor_copy(y[:], accs[nt][:])
             nc.sync.dma_start(out_0[P * nt : P * (nt + 1), :], y[:])
         store_page_scales(1, page_scales)

from contextlib import ExitStack

import concourse.mybir as mybir

K, T, S, H, T2, PM, N = 1024, 4096, 1024, 1024, 2048, 512, 512
FLOPS = 2 * K * H * S + 2 * 2 * H * N * PM

F32 = mybir.dt.float32
BF16 = mybir.dt.bfloat16
I32 = mybir.dt.int32
U32 = mybir.dt.uint32
U16 = mybir.dt.uint16
U8 = mybir.dt.uint8
FP8X4 = mybir.dt.float8_e4m3fn_x4
FP4X4 = mybir.dt.float4_e2m1fn_x4
ACT = mybir.ActivationFunctionType
ALU = mybir.AluOpType

P = 128
PACK = 4
PASS = P * PACK
GROUPS = H // PASS
TILES = GROUPS * PACK
QUADS = 4
BANK = 512
CHUNK = 512
CHUNKS = T2 // CHUNK
N_TILES = N // P
AHEAD = 2

KB = 1024
TAB = 0
W1_FIRST = 32 * KB
W1_SECOND = 48 * KB
REGROUPED_SECOND = W1_FIRST + 8 * KB
PAGES = 64 * KB
WGS_SECOND = 96 * KB
LATE_SCALES = 100 * KB
HS = 104 * KB
W2_RAW = 144 * KB
WOVEN = 160 * KB
TAB_SCALES = 176 * KB
PICKED = 180 * KB
STAGING = 189 * KB
W1_CODES = 197 * KB
W2_CODES = 207 * KB
WM = 211 * KB
X_FIRST = 214 * KB
ABS = 222 * KB
MOON_FIRST = 230 * KB

ROWS_BYTES = 8 * KB
H_BYTES = 4 * KB
WORDS_BYTES = 2 * KB
PLANE_BYTES = 512

PAGE_AT = [PAGES + i * ROWS_BYTES for i in range(PACK)] + [HS + i * ROWS_BYTES for i in range(PACK)]
H_AT = [HS + slot * H_BYTES for slot in (0, 2, 1, 3, 4, 6, 8, 9)]
FIRST_TANH_AT = WOVEN + 6 * KB
MAG_AT = [
    ABS, ABS + H_BYTES, W1_SECOND + ROWS_BYTES, W1_SECOND + ROWS_BYTES,
    W2_RAW + ROWS_BYTES, ABS + H_BYTES, ABS, FIRST_TANH_AT,
]
TANH_AT = 4 * [FIRST_TANH_AT] + 3 * [TAB] + [W1_SECOND]


def tile_list_auroral_arc_page_kernel(
    tc, tab_words, tab_scales, offs, w1, lift, page0, wgs, offs2, offs3, ease, tgain, moon, w2,
    wm_words, wm_scales, out_0, out_1, out_2, out_3,
):
    nc = tc.nc
    with ExitStack() as ctx:
        lists = ctx.enter_context(tc.tile_pool(name="lists", bufs=1))
        sb = ctx.enter_context(tc.tile_pool(name="sb", bufs=1))
        psum = ctx.enter_context(tc.psum_pool(name="psum", bufs=1))

        def place(name, shape, dtype, offset):
            return sb.tile(shape, dtype, name=name, offset=offset, align_bytes=64)

        def rows_4p_t(matrix, g):
            return matrix[PASS * g : PASS * (g + 1), :].rearrange("(p t) c -> p t c", t=PACK)

        def load_rows(name, matrix, g, cols, offset):
            raw = place(name, [P, PACK, 512], F32, offset)
            nc.sync.dma_start(raw[:], rows_4p_t(matrix, g)[:, :, cols])
            return raw

        def load_per_row(tile, vector):
            nc.sync.dma_start(tile[:], vector.rearrange("(g p t) -> p g t", g=GROUPS, t=PACK))

        def load_wgs(queue, tile, ts):
            dealt = wgs.rearrange("(q t) j -> q t j", t=PACK)[:, ts, :]
            for quad in range(QUADS):
                queue.dma_start(tile[32 * quad : 32 * (quad + 1), :, :], dealt)

        pages = {}

        def load_page(i):
            g, t = divmod(i, PACK)
            pages[i] = place(f"page{i}", [P, T2], F32, PAGE_AT[i])
            nc.sync.dma_start(pages[i][:], rows_4p_t(page0, g)[:, t, :])

        def quantize(name, woven, words_at, scales_at):
            width = woven.shape[1] // PACK
            words = place(name + "_words", [P, width], I32, words_at)
            scales = place(name + "_scales", [P, width], U8, scales_at)
            nc.vector.quantize_mx(words[:].bitcast(FP8X4), scales[:], woven[:])
            return words, scales

        def by_four_columns(rows):
            return rows.rearrange("p t (c i) -> p c t i", i=4)

        def woven_by_four_columns(woven):
            return woven.rearrange("p (c i t) -> p c t i", i=4, t=PACK)

        def weave(woven, rows):
            nc.scalar.copy(woven_by_four_columns(woven)[:, :, 0 : rows.shape[1], :], by_four_columns(rows))

        idx = lists.tile([P, S // 16], U16, name="idx")
        idx2 = lists.tile([P, S // 16], U16, name="idx2")
        idx3 = lists.tile([P, PM // 16], U16, name="idx3")
        lift_sb = lists.tile([P, GROUPS, PACK], F32, name="lift_sb")
        ease_sb = lists.tile([P, GROUPS, PACK], F32, name="ease_sb")
        tgain_sb = lists.tile([P, GROUPS, PACK], F32, name="tgain_sb")

        nc.sync.dma_start(idx[:], offs)
        tab = []
        for a in range(GROUPS):
            words = place(f"tab{a}", [P, T], I32, TAB + a * 4 * T)
            nc.sync.dma_start(words[:], tab_words[a].rearrange("p c i -> p (c i)").bitcast(I32))
            tab.append(words)
            if a == 0:
                tab_sc = place("tab_sc", [P, T], U8, TAB_SCALES)
                nc.vector.memset(tab_sc[:].bitcast(I32), 0)
                for quad in range(QUADS):
                    nc.sync.dma_start(
                        tab_sc[32 * quad : 32 * quad + 8, :].bitcast(I32),
                        tab_scales[:, 4 * quad : 4 * quad + 4, :].bitcast(I32),
                    )

        w1_raw = {}
        for a in range(GROUPS):
            w1_raw[0, a] = load_rows(f"w1_raw0{a}", w1, a, slice(0, PASS), W1_FIRST + a * ROWS_BYTES)
        load_per_row(lift_sb, lift)
        nc.sync.dma_start(idx2[:], offs2)
        load_page(0)
        nc.sync.dma_start(idx3[:], offs3)
        load_page(1)
        wgs_second = place("wgs_second", [P, 1, S], F32, WGS_SECOND)
        load_wgs(nc.sync, wgs_second, slice(1, 2))
        for a in range(GROUPS):
            w1_raw[1, a] = load_rows(f"w1_raw1{a}", w1, a, slice(PASS, H), W1_SECOND + a * ROWS_BYTES)
        w2_raw = [load_rows(f"w2_raw{g}", w2, g, slice(0, N), W2_RAW + g * ROWS_BYTES) for g in range(GROUPS)]
        load_page(2)
        load_per_row(ease_sb, ease)
        load_per_row(tgain_sb, tgain)

        wm = place("wm", [P, GROUPS, 2 * N], U8, WM)
        wm_sc = place("wm_sc", [P, GROUPS, N], U8, WM + GROUPS * 2 * N)
        nc.vector.memset(wm_sc[:].bitcast(I32), 0)
        for quad in range(QUADS):
            nc.sync.dma_start(
                wm_sc[32 * quad : 32 * quad + 4, :, :].bitcast(I32),
                wm_scales[:, 4 * quad : 4 * quad + 4, :].rearrange("a r c -> r a c").bitcast(I32),
            )

        picked = []
        picked_sc = place("picked_sc", [P, S], U8, PICKED + GROUPS * H_BYTES)
        for a in range(GROUPS):
            words = place(f"picked{a}", [P, S], U32, PICKED + a * H_BYTES)
            nc.vector.tensor_copy(words[:], tab[a][:].bitcast(U32).indirect(idx[:]))
            picked.append(words)
            if a == 0:
                nc.vector.tensor_copy(picked_sc[:], tab_sc[:].indirect(idx[:]))
        wgs_first = place("wgs_first", [P, 1, S], F32, TAB_SCALES)
        load_wgs(nc.scalar, wgs_first, slice(0, 1))

        def weave_w1(copy, g, a):
            woven = place(f"w1_woven{g}{a}", [P, PACK * PASS], BF16, STAGING + a * H_BYTES)
            copy(
                woven[:].rearrange("p (t m j) -> p m j t", t=PACK, j=PACK),
                w1_raw[g, a][:].rearrange("p j (m t) -> p m j t", t=PACK),
            )
            return woven

        w1q = {}
        for a in range(GROUPS):
            woven = weave_w1(nc.vector.tensor_copy, 0, a)
            w1q[0, a] = quantize(
                f"w1q0{a}", woven, W1_CODES + a * WORDS_BYTES, W1_CODES + 4 * WORDS_BYTES + a * PLANE_BYTES
            )

        wgs_rest = place("wgs_rest", [P, 2, S], F32, W1_FIRST)
        load_wgs(nc.gpsimd, wgs_rest, slice(2, 4))
        gains = [wgs_first[:, 0, :], wgs_second[:, 0, :], wgs_rest[:, 0, :], wgs_rest[:, 1, :]]

        banks = [psum.tile([P, BANK], F32, name=f"strip{b}") for b in range(4)]
        accs = [psum.tile([P, PM], F32, name=f"acc{nt}") for nt in range(N_TILES)]
        halves = [slice(half * BANK, (half + 1) * BANK) for half in range(S // BANK)]
        hs = {}

        def make_h(i):
            g, t = divmod(i, PACK)
            mag = place(f"mag{i}", [P, S], F32, MAG_AT[i])
            hs[i] = place(f"h{i}", [P, S], F32, H_AT[i])
            row_lift = lift_sb[:, g, t : t + 1]
            for half, cols in enumerate(halves):
                bank = banks[2 * (i % 2) + half]
                for a in range(GROUPS):
                    words, scales = w1q[g, a]
                    nc.tensor.matmul_mx(
                        bank[:],
                        lhsT=words[:, t * P : (t + 1) * P].bitcast(FP8X4),
                        lhsT_scale=scales[:, t * P : (t + 1) * P],
                        rhs=picked[a][:, cols].bitcast(FP8X4),
                        rhs_scale=picked_sc[4 * a :, cols],
                        start=(a == 0),
                        stop=(a == GROUPS - 1),
                    )
                nc.scalar.activation(mag[:, cols], bank[:], ACT.Abs)
                if i == 0:
                    nc.scalar.activation(hs[i][:, cols], mag[:, cols], ACT.Sqrt, bias=row_lift)
            if i > 0:
                nc.scalar.activation(hs[i][:], mag[:], ACT.Sqrt, bias=row_lift)

        make_h(0)
        make_h(1)
        load_page(3)
        nc.sync.dma_start(wm[:].bitcast(I32), wm_words.rearrange("a p c -> p a c").bitcast(I32))
        w1_woven = [weave_w1(nc.scalar.copy, 1, a) for a in range(GROUPS)]
        make_h(2)
        make_h(3)
        moons = [load_rows("moon0", moon, 0, slice(0, PM), MOON_FIRST)]

        xs = {}

        def scatter_and_fetch(i):
            g, t = divmod(i, PACK)
            page = pages[i]
            if i == 0:
                for cols in halves:
                    entries = idx2[:, cols.start // 16 : cols.stop // 16]
                    nc.vector.tensor_tensor(page[:].indirect(entries), hs[i][:, cols], gains[t][:, cols], ALU.mult)
            else:
                nc.vector.tensor_tensor(page[:].indirect(idx2[:]), hs[i][:], gains[t], ALU.mult)
            if AHEAD <= i < TILES - AHEAD:
                load_page(i + AHEAD)
            if t == 0:
                xs[g] = place(f"x{g}", [P, PACK, PM], F32, X_FIRST if g == 0 else W2_RAW)
            nc.vector.tensor_copy(xs[g][:, t, :], page[:].indirect(idx3[:]))

        regrouped = {}

        def regroup(i):
            g, t = divmod(i, PACK)
            queue = nc.gpsimd if g == 0 else nc.sync
            queue.dma_start(regrouped[g][:, t, :], pages[i][:])

        def store_page(i):
            g, t = divmod(i, PACK)
            nc.sync.dma_start(rows_4p_t(out_1, g)[:, t, :], pages[i][:])

        arcs = {}

        def make_arc(i):
            g, t = divmod(i, PACK)
            if t == 0:
                arcs[g] = place(f"arc{g}", [P, PM * PACK], BF16, STAGING if g == 0 else PICKED)
            bent = place(f"bent{i}", [P, PM], F32, TANH_AT[i])
            nc.scalar.activation(bent[:], xs[g][:, t, :], ACT.Tanh, scale=ease_sb[:, g, t : t + 1])
            nc.scalar.activation(
                arcs[g][:].rearrange("p (m t) -> p m t", t=PACK)[:, :, t], bent[:], ACT.Copy,
                scale=tgain_sb[:, g, t : t + 1],
            )

        def make_lit(g):
            lit = place(f"lit{g}", [P, PM * PACK], BF16, (STAGING if g == 0 else PICKED) + H_BYTES)
            nc.vector.tensor_tensor(
                woven_by_four_columns(lit[:]), by_four_columns(xs[g][:]), by_four_columns(moons[g][:]), ALU.add
            )
            return lit

        def moon_passes(g, litq):
            for nt in range(N_TILES):
                nc.tensor.matmul_mx(
                    accs[nt][:],
                    lhsT=wm[:, g, 2 * P * nt : 2 * P * (nt + 1)].bitcast(FP4X4),
                    lhsT_scale=wm_sc[:, g, P * nt : P * (nt + 1)],
                    rhs=litq[0][:].bitcast(FP8X4),
                    rhs_scale=litq[1][:],
                    start=(g == 0),
                    stop=False,
                )

        def arc_passes(g, arcq):
            words, scales = w2q[g]
            for nt in range(N_TILES):
                nc.tensor.matmul_mx(
                    accs[nt][:],
                    lhsT=words[:, P * nt : P * (nt + 1)].bitcast(FP8X4),
                    lhsT_scale=scales[:, P * nt : P * (nt + 1)],
                    rhs=arcq[0][:].bitcast(FP8X4),
                    rhs_scale=arcq[1][:],
                    start=False,
                    stop=(g == GROUPS - 1),
                )

        def weave_page(g, offset):
            woven = place(f"woven_page{g}", [P, PACK * T2], BF16, offset)
            chunks = [woven[:, PACK * c * CHUNK : PACK * (c + 1) * CHUNK] for c in range(CHUNKS)]
            for c in range(CHUNKS):
                weave(chunks[c], regrouped[g][:, :, c * CHUNK : (c + 1) * CHUNK])
            return chunks

        def weave_last_tile(chunks, c):
            nc.scalar.copy(
                chunks[c].rearrange("p (m t) -> p m t", t=PACK)[:, :, PACK - 1],
                pages[TILES - 1][:, c * CHUNK : (c + 1) * CHUNK],
            )

        def quantize_page_chunk(g, c, chunks, scales, words_at):
            words = place(f"page_words{g}{c}", [P, CHUNK], I32, words_at + c * WORDS_BYTES)
            cols = slice(c * CHUNK, (c + 1) * CHUNK)
            nc.vector.quantize_mx(words[:].bitcast(FP8X4), scales[:, cols], chunks[c])
            nc.sync.dma_start(out_2[g][:, cols, :].rearrange("p m t -> p (m t)").bitcast(I32), words[:])

        def store_page_scales(g, scales):
            for quad in range(QUADS):
                nc.sync.dma_start(
                    out_3[g][4 * quad : 4 * quad + 4, :].bitcast(I32),
                    scales[32 * quad : 32 * quad + 4, :].bitcast(I32),
                )

        scatter_and_fetch(0)
        regrouped[0] = place("regrouped0", [P, PACK, T2], F32, TAB)
        regroup(0)
        scatter_and_fetch(1)
        regroup(1)
        for a in range(GROUPS):
            w1q[1, a] = quantize(
                f"w1q1{a}", w1_woven[a], W1_CODES + (GROUPS + a) * WORDS_BYTES, H_AT[1] + a * PLANE_BYTES
            )
        w2_woven = []
        for g in range(GROUPS):
            woven = place(f"w2_woven{g}", [P, PACK * N], BF16, WOVEN + g * 3 * H_BYTES)
            weave(woven[:], w2_raw[g][:])
            w2_woven.append(woven)
        for i in range(PACK, TILES):
            make_h(i)
        scatter_and_fetch(2)
        regroup(2)
        w2q = [
            quantize(f"w2q{g}", w2_woven[g], W2_CODES + g * WORDS_BYTES, LATE_SCALES + 3 * KB + g * PLANE_BYTES)
            for g in range(GROUPS)
        ]
        for i in range(3):
            make_arc(i)
        scatter_and_fetch(3)
        regroup(3)
        moons.append(load_rows("moon1", moon, 1, slice(0, PM), PAGE_AT[3]))
        nc.gpsimd.dma_start(rows_4p_t(out_1, 0), regrouped[0][:])
        lit = make_lit(0)
        make_arc(3)
        chunks = weave_page(0, WOVEN)

        scatter_and_fetch(4)
        regrouped[1] = place("regrouped1", [P, PACK - 1, T2], F32, REGROUPED_SECOND)
        regroup(4)
        litq = quantize("litq0", lit, W1_CODES + 3 * WORDS_BYTES, PAGE_AT[4])
        arcq = quantize("arcq0", arcs[0], W2_RAW + ROWS_BYTES + WORDS_BYTES, PAGE_AT[4] + PLANE_BYTES)
        moon_passes(0, litq)
        arc_passes(0, arcq)
        make_arc(4)
        scatter_and_fetch(5)
        regroup(5)
        nc.sync.dma_start(rows_4p_t(out_1, 1)[:, 0:2, :], regrouped[1][:, 0:2, :])
        page_scales = place("page_scales0", [P, T2], U8, PAGE_AT[5])
        for c in range(CHUNKS):
            quantize_page_chunk(0, c, chunks, page_scales, PAGE_AT[0])
        store_page_scales(0, page_scales)
        make_arc(5)
        scatter_and_fetch(6)
        regroup(6)
        store_page(6)
        make_arc(6)
        chunks = weave_page(1, TAB)
        scatter_and_fetch(7)
        store_page(7)

        weave_last_tile(chunks, 0)
        lit = make_lit(1)
        make_arc(7)
        litq = quantize("litq1", lit, W2_RAW + ROWS_BYTES + 2 * WORDS_BYTES, LATE_SCALES + T2)
        moon_passes(1, litq)
        page_scales = place("page_scales1", [P, T2], U8, LATE_SCALES)
        quantize_page_chunk(1, 0, chunks, page_scales, PAGE_AT[1])
        arcq = quantize("arcq1", arcs[1], W2_RAW + ROWS_BYTES + 3 * WORDS_BYTES, LATE_SCALES + T2 + PLANE_BYTES)
        arc_passes(1, arcq)
        for c in range(1, CHUNKS):
            weave_last_tile(chunks, c)
        for nt in range(N_TILES):
            if nt > 0:
                quantize_page_chunk(1, nt, chunks, page_scales, PAGE_AT[1])
            y = place(f"y{nt}", [P, PM], F32, PAGE_AT[2] + nt * 4 * PM)
            nc.vector.tensor_copy(y[:], accs[nt][:])
            nc.sync.dma_start(out_0[P * nt : P * (nt + 1), :], y[:])
        store_page_scales(1, page_scales)
